import numpy as np
import ml_dtypes


def mxq(x, axis, fmt="e4m3"):
    dtype, down = {"e4m3": (ml_dtypes.float8_e4m3fn, 7), "e5m2": (ml_dtypes.float8_e5m2, 14)}[fmt]
    v = np.moveaxis(np.asarray(x, np.float32).astype(ml_dtypes.bfloat16).astype(np.float64), axis, -1)
    blocks = v.reshape(v.shape[:-1] + (-1, 32))
    amax = np.abs(blocks).max(-1, keepdims=True)
    byte = np.maximum(np.where(amax > 0, np.frexp(amax)[1] - 1 + 127, 0) - down, 1)
    scale = np.exp2(byte - 127.0)
    codes = (blocks / scale).astype(np.float32).astype(dtype).astype(np.float64)
    return np.moveaxis((codes * scale).reshape(v.shape), -1, axis)


WIDE = False


def mx_kscale(k):
    if not WIDE:
        return np.ones(k)
    levels = np.array([30, -30])
    if k % 512:
        return np.exp2(np.random.permutation(np.resize(levels, k // 32))).repeat(32)
    a = np.empty((k // 512, 16))
    for p in range(k // 512):
        a[p, :8] = np.random.permutation(np.resize(levels, 8))
        for g in range(8):
            far = levels[np.abs(levels - a[p, g]) >= 10]
            a[p, g + 8] = far[np.random.randint(len(far))]
    return np.exp2(a.ravel()).repeat(32)


def f64(x):
    return np.asarray(x).astype(np.float64)


def striped(idx):
    return np.tile(np.asarray(idx).reshape(-1, 16).T, (8, 1)).astype(np.uint16)


def unstriped(offs):
    return offs[:16].T.reshape(-1).astype(np.int64)


E2M1 = np.array([0.0, 0.5, 1.0, 1.5, 2.0, 3.0, 4.0, 6.0, -0.0, -0.5, -1.0, -1.5, -2.0, -3.0, -4.0, -6.0])


def pack_weight(w, fmt):
    k, n = w.shape
    w = f64(np.asarray(w, np.float32).astype(ml_dtypes.bfloat16)).reshape(k // 32, 32, n)
    amax = np.abs(w).max(1)
    if fmt in ("e4m3", "e5m2"):
        byte = np.frexp(amax)[1] - 1 + 127 - (7 if fmt == "e4m3" else 14)
    else:
        mant, ex = np.frexp(amax / 6.0)
        byte = np.where(mant > 0.5, ex, ex - 1) + 127
    byte = np.clip(np.where(amax > 0, byte, 1), 1, 254)
    scaled = (w * np.exp2(127.0 - byte)[:, None, :]).reshape(k, n).astype(np.float32)
    by_word = np.ascontiguousarray(scaled.reshape(k // 512, 128, 4, n).transpose(0, 1, 3, 2))
    if fmt in ("e4m3", "e5m2"):
        words = by_word.astype(ml_dtypes.float8_e4m3fn if fmt == "e4m3" else ml_dtypes.float8_e5m2).view(np.uint8)
    else:
        c = by_word.astype(ml_dtypes.float4_e2m1fn).view(np.uint8) & 0xF
        words = (c[..., 0::2] | (c[..., 1::2] << 4)).reshape(k // 512, 128, 2 * n)
    return np.ascontiguousarray(words), np.ascontiguousarray(byte.astype(np.uint8).reshape(k // 512, 16, n))


def unpack_weight(words, scales, fmt):
    g, _, n = scales.shape
    words = np.ascontiguousarray(words).reshape(g, 128, n, -1)
    if fmt in ("e4m3", "e5m2"):
        vals = words.view(ml_dtypes.float8_e4m3fn if fmt == "e4m3" else ml_dtypes.float8_e5m2).astype(np.float64)
    else:
        nib = np.empty((g, 128, n, 4), np.uint8)
        nib[..., 0::2] = words & 0xF
        nib[..., 1::2] = words >> 4
        vals = E2M1[nib]
    vals = vals * np.repeat(np.exp2(scales.astype(np.float64) - 127.0), 8, axis=1)[..., None]
    return vals.transpose(0, 1, 3, 2).reshape(g * 512, n)


def sigmoid(v):
    return 1.0 / (1.0 + np.exp(-v))


K, T, J, R, Q, N = 512, 1024, 256, 512, 1024, 256


def setup_inputs():
    n = np.random.standard_normal
    idx = np.random.permutation(T)[:J]
    idx2 = np.random.permutation(Q)[:J]
    fk = mx_kscale(K)
    fr = mx_kscale(R)
    xtp = pack_weight(n((K, T)) / fk[:, None], "e2m1")
    wp = pack_weight(n((K, R)) * 1 / np.sqrt(K) * fk[:, None] * fr, "e4m3")
    w2p = pack_weight(n((K, R)) * 1 / np.sqrt(K) * fk[:, None] * fr, "e5m2")
    wbp = pack_weight(n((R, N)) * 1 / np.sqrt(R) / fr[:, None], "e2m1")
    return {
        "xt_words": xtp[0],
        "xt_scales": xtp[1],
        "w_words": wp[0],
        "w_scales": wp[1],
        "w2_words": w2p[0],
        "w2_scales": w2p[1],
        "tg": (1.0 * n((R, Q))).astype(np.float32),
        "sg": (np.random.uniform(0.6, 1.6, (R, 1))).astype(np.float32),
        "bg": (np.random.uniform(-1.0, 1.0, (R, 1))).astype(np.float32),
        "wb_words": wbp[0],
        "wb_scales": wbp[1],
        "offs": striped(idx),
        "offs2": striped(idx2),
    }


def reference(xt_words, xt_scales, w_words, w_scales, w2_words, w2_scales, tg, sg, bg, wb_words, wb_scales, offs, offs2):
    idx = unstriped(offs)
    idx2 = unstriped(offs2)
    xtu = unpack_weight(xt_words, xt_scales, "e2m1")
    wu = unpack_weight(w_words, w_scales, "e4m3")
    w2u = unpack_weight(w2_words, w2_scales, "e5m2")
    wbu = unpack_weight(wb_words, wb_scales, "e2m1")
    xtidxg = xtu[:, idx]
    a = wu.T @ xtidxg
    b = w2u.T @ xtidxg
    hid = np.abs(a - b) * sigmoid(f64(tg)[:, idx2] * f64(sg) + f64(bg))
    hidq = mxq(hid, 0, "e5m2")
    y = wbu.T @ hidq
    return y

@@ -1,0 +1,157 @@
+from contextlib import ExitStack
+
+import concourse.mybir as mybir
+
+K, T, J, R, Q, N = 512, 1024, 256, 512, 1024, 256
+FLOPS = 2 * (2 * K * R * J + R * N * J)
+
+F32 = mybir.dt.float32
+BF16 = mybir.dt.bfloat16
+I32 = mybir.dt.int32
+U32 = mybir.dt.uint32
+U16 = mybir.dt.uint16
+U8 = mybir.dt.uint8
+E4M3 = mybir.dt.float8_e4m3fn_x4
+E5M2 = mybir.dt.float8_e5m2_x4
+E2M1 = mybir.dt.float4_e2m1fn_x4
+ACT = mybir.ActivationFunctionType
+ALU = mybir.AluOpType
+
+P = 128
+PACK = 4
+
+
+def load_scales(queue, plane, rows, which=range(4)):
+    for r in which:
+        queue.dma_start(out=plane[r:P:32, :].bitcast(I32), in_=rows[0, r:16:4, :].bitcast(I32))
+
+
+def tile_list_twow_tablegate_one_plain_kernel(
+    tc, xt_words, xt_scales, w_words, w_scales, w2_words, w2_scales, tg, sg, bg, wb_words, wb_scales, offs, offs2, out
+):
+    nc = tc.nc
+    with ExitStack() as ctx:
+        sb = ctx.enter_context(tc.tile_pool(name="sb", bufs=1))
+        ps = ctx.enter_context(tc.psum_pool(name="ps", bufs=1))
+
+        tok_list = sb.tile([P, J // 16], U16, name="tok_list")
+        gate_list = sb.tile([P, J // 16], U16, name="gate_list")
+        xt_w = sb.tile([P, T], U16, name="xt_w", align_bytes=64)
+        xt_s = sb.tile([P, T], U8, name="xt_s", align_bytes=64)
+        w_w = sb.tile([P, R], U32, name="w_w", align_bytes=64)
+        w_s = sb.tile([P, R], U8, name="w_s", align_bytes=64)
+        w2_w = sb.tile([P, R], U32, name="w2_w", align_bytes=64)
+        w2_s = sb.tile([P, R], U8, name="w2_s", align_bytes=64)
+        wb_w = sb.tile([P, 2 * N], U8, name="wb_w", align_bytes=64)
+        wb_s = sb.tile([P, N], U8, name="wb_s", align_bytes=64)
+        slope = sb.tile([P, PACK], F32, name="slope")
+        offset = sb.tile([P, PACK], F32, name="offset")
+        table = [sb.tile([P, Q], F32, name="table%d" % t) for t in range(PACK)]
+
+        for plane in (xt_s, w_s, w2_s, wb_s):
+            nc.vector.memset(plane[:].bitcast(I32), 0)
+
+        tg_rows = tg.rearrange("(p t) q -> p t q", t=PACK)
+        nc.gpsimd.dma_start(out=slope[:], in_=sg.rearrange("(p t) o -> p (t o)", t=PACK))
+        nc.gpsimd.dma_start(out=offset[:], in_=bg.rearrange("(p t) o -> p (t o)", t=PACK))
+        nc.sync.dma_start(tok_list[:], offs)
+        nc.sync.dma_start(out=xt_w[:].bitcast(I32), in_=xt_words[0].bitcast(I32))
+        nc.sync.dma_start(out=w_w[:].bitcast(I32), in_=w_words[0].rearrange("p n t -> p (n t)").bitcast(I32))
+        load_scales(nc.sync, xt_s, xt_scales)
+        nc.sync.dma_start(out=w2_w[:].bitcast(I32), in_=w2_words[0].rearrange("p n t -> p (n t)").bitcast(I32))
+        nc.sync.dma_start(out=table[0][:], in_=tg_rows[:, 0, :])
+        load_scales(nc.sync, w_s, w_scales)
+        nc.sync.dma_start(gate_list[:], offs2)
+        load_scales(nc.sync, w2_s, w2_scales, range(0, 1))
+        nc.sync.dma_start(out=table[1][:], in_=tg_rows[:, 1, :])
+        load_scales(nc.sync, w2_s, w2_scales, range(1, 4))
+        nc.sync.dma_start(out=table[2][:], in_=tg_rows[:, 2, :])
+        nc.sync.dma_start(out=table[3][:], in_=tg_rows[:, 3, :])
+        nc.sync.dma_start(out=wb_w[:].bitcast(I32), in_=wb_words[0].bitcast(I32))
+        load_scales(nc.sync, wb_s, wb_scales)
+
+        xg_w = sb.tile([P, J], U16, name="xg_w", align_bytes=64)
+        xg_s = sb.tile([P, J], U8, name="xg_s", align_bytes=64)
+        w_wd = sb.tile([P, PACK, P], U32, name="w_wd", align_bytes=64)
+        w_sd = sb.tile([P, PACK, P], U8, name="w_sd", align_bytes=64)
+        w2_wd = sb.tile([P, PACK, P], U32, name="w2_wd", align_bytes=64)
+        w2_sd = sb.tile([P, PACK, P], U8, name="w2_sd", align_bytes=64)
+
+        def deal(dst, src):
+            nc.vector.tensor_copy(out=dst, in_=src.rearrange("p (m t) -> p t m", t=PACK))
+
+        nc.vector.tensor_copy(out=xg_w[:], in_=xt_w[:].indirect(tok_list[:]))
+        deal(w_wd[:].bitcast(I32), w_w[:].bitcast(I32))
+        nc.vector.tensor_copy(out=xg_s[:], in_=xt_s[:].indirect(tok_list[:]))
+        deal(w2_wd[:].bitcast(I32), w2_w[:].bitcast(I32))
+        deal(w_sd[:], w_s[:])
+        deal(w2_sd[:], w2_s[:])
+
+        gate = [sb.tile([P, 2, J], F32, name="gate%d" % u) for u in range(2)]
+
+        def look(t):
+            nc.scalar.activation(
+                out=gate[t // 2][:, t % 2, :],
+                in_=table[t][:].indirect(gate_list[:]),
+                func=ACT.Sigmoid,
+                bias=offset[:, t : t + 1],
+                scale=slope[:, t : t + 1],
+            )
+
+        look(0)
+        look(1)
+
+        a_ps = [ps.tile([P, 2, J], F32, name="a_ps%d" % u) for u in range(2)]
+        b_ps = [ps.tile([P, 2, J], F32, name="b_ps%d" % u) for u in range(2)]
+        a_sb = [sb.tile([P, 2, J], F32, name="a_sb%d" % u) for u in range(2)]
+        d_sb = [sb.tile([P, 2, J], F32, name="d_sb%d" % u) for u in range(2)]
+        mag = [sb.tile([P, J, 2], F32, name="mag%d" % u) for u in range(2)]
+        hid = sb.tile([P, J, PACK], BF16, name="hid", align_bytes=64)
+
+        for acc, words, plane, fmt in ((a_ps, w_wd, w_sd, E4M3), (b_ps, w2_wd, w2_sd, E5M2)):
+            for u in range(2):
+                for e in range(2):
+                    nc.tensor.matmul_mx(
+                        out=acc[u][:, e, :],
+                        lhsT=words[:, 2 * u + e, :].bitcast(fmt),
+                        lhsT_scale=plane[:, 2 * u + e, :],
+                        rhs=xg_w[:].bitcast(E2M1),
+                        rhs_scale=xg_s[:],
+                        start=True,
+                        stop=True,
+                    )
+        for u in range(2):
+            nc.scalar.copy(out=a_sb[u][:], in_=a_ps[u][:])
+        for u in range(2):
+            nc.vector.tensor_tensor(out=d_sb[u][:], in0=a_sb[u][:], in1=b_ps[u][:], op=ALU.subtract)
+            nc.scalar.activation(out=mag[u][:], in_=d_sb[u][:].rearrange("p e j -> p j e"), func=ACT.Abs)
+            look(2 + u)
+        for u in range(2):
+            nc.vector.tensor_tensor(
+                out=hid[:, :, 2 * u : 2 * u + 2],
+                in0=mag[u][:],
+                in1=gate[u][:].rearrange("p e j -> p j e"),
+                op=ALU.mult,
+            )
+        hq_w = sb.tile([P, J], U32, name="hq_w", align_bytes=64)
+        hq_s = sb.tile([P, J], U8, name="hq_s", align_bytes=64)
+        nc.vector.quantize_mx(out=hq_w[:].bitcast(E5M2), scales=hq_s[:], in_=hid[:].rearrange("p j t -> p (j t)"))
+
+        for h in range(2):
+            y_ps = ps.tile([P, J], F32, name="y_ps%d" % h)
+            y_sb = sb.tile([P, J], F32, name="y_sb%d" % h)
+            nc.tensor.matmul_mx(
+                out=y_ps[:],
+                lhsT=wb_w[:, 2 * h * P : 2 * (h + 1) * P].bitcast(E2M1),
+                lhsT_scale=wb_s[:, h * P : (h + 1) * P],
+                rhs=hq_w[:].bitcast(E5M2),
+                rhs_scale=hq_s[:],
+                start=True,
+                stop=True,
+            )
+            if h == 0:
+                nc.vector.tensor_copy(out=y_sb[:], in_=y_ps[:])
+                nc.sync.dma_start(out=out[h * P : (h + 1) * P, :], in_=y_sb[:])
+            else:
+                nc.scalar.copy(out=y_sb[:], in_=y_ps[:])
+                nc.scalar.dma_start(out=out[h * P : (h + 1) * P, :], in_=y_sb[:])

@@ -48,6 +48,10 @@ def tile_list_twow_tablegate_one_plain_kernel(
         offset = sb.tile([P, PACK], F32, name="offset")
         table = [sb.tile([P, Q], F32, name="table%d" % t) for t in range(PACK)]
 
+        warm_in = sb.tile([P, 1], F32, name="warm_in")
+        warm_out = sb.tile([P, 1], F32, name="warm_out")
+        nc.gpsimd.memset(warm_in[:], 0.0)
+        nc.scalar.activation(out=warm_out[:], in_=warm_in[:], func=ACT.Sigmoid)
         for plane in (xt_s, w_s, w2_s, wb_s):
             nc.vector.memset(plane[:].bitcast(I32), 0)
 

@@ -46,7 +46,7 @@ def tile_list_twow_tablegate_one_plain_kernel(
         wb_s = sb.tile([P, N], U8, name="wb_s", align_bytes=64)
         slope = sb.tile([P, PACK], F32, name="slope")
         offset = sb.tile([P, PACK], F32, name="offset")
-        table = [sb.tile([P, Q], F32, name="table%d" % t) for t in range(PACK)]
+        table = [sb.tile([P, Q], F32, name="table%d" % t, tag="table%d" % t) for t in range(PACK)]
 
         warm_in = sb.tile([P, 1], F32, name="warm_in")
         warm_out = sb.tile([P, 1], F32, name="warm_out")
@@ -58,17 +58,16 @@ def tile_list_twow_tablegate_one_plain_kernel(
         tg_rows = tg.rearrange("(p t) q -> p t q", t=PACK)
         nc.gpsimd.dma_start(out=slope[:], in_=sg.rearrange("(p t) o -> p (t o)", t=PACK))
         nc.gpsimd.dma_start(out=offset[:], in_=bg.rearrange("(p t) o -> p (t o)", t=PACK))
-        nc.sync.dma_start(tok_list[:], offs)
         nc.sync.dma_start(out=xt_w[:].bitcast(I32), in_=xt_words[0].bitcast(I32))
-        nc.sync.dma_start(out=w_w[:].bitcast(I32), in_=w_words[0].rearrange("p n t -> p (n t)").bitcast(I32))
+        nc.sync.dma_start(tok_list[:], offs)
         load_scales(nc.sync, xt_s, xt_scales)
-        nc.sync.dma_start(out=w2_w[:].bitcast(I32), in_=w2_words[0].rearrange("p n t -> p (n t)").bitcast(I32))
+        nc.sync.dma_start(out=w_w[:].bitcast(I32), in_=w_words[0].rearrange("p n t -> p (n t)").bitcast(I32))
         nc.sync.dma_start(out=table[0][:], in_=tg_rows[:, 0, :])
         load_scales(nc.sync, w_s, w_scales)
+        nc.sync.dma_start(out=w2_w[:].bitcast(I32), in_=w2_words[0].rearrange("p n t -> p (n t)").bitcast(I32))
         nc.sync.dma_start(gate_list[:], offs2)
-        load_scales(nc.sync, w2_s, w2_scales, range(0, 1))
         nc.sync.dma_start(out=table[1][:], in_=tg_rows[:, 1, :])
-        load_scales(nc.sync, w2_s, w2_scales, range(1, 4))
+        load_scales(nc.sync, w2_s, w2_scales)
         nc.sync.dma_start(out=table[2][:], in_=tg_rows[:, 2, :])
         nc.sync.dma_start(out=table[3][:], in_=tg_rows[:, 3, :])
         nc.sync.dma_start(out=wb_w[:].bitcast(I32), in_=wb_words[0].bitcast(I32))
@@ -77,19 +76,20 @@ def tile_list_twow_tablegate_one_plain_kernel(
         xg_w = sb.tile([P, J], U16, name="xg_w", align_bytes=64)
         xg_s = sb.tile([P, J], U8, name="xg_s", align_bytes=64)
         w_wd = sb.tile([P, PACK, P], U32, name="w_wd", align_bytes=64)
-        w_sd = sb.tile([P, PACK, P], U8, name="w_sd", align_bytes=64)
         w2_wd = sb.tile([P, PACK, P], U32, name="w2_wd", align_bytes=64)
-        w2_sd = sb.tile([P, PACK, P], U8, name="w2_sd", align_bytes=64)
+        w_sd = [sb.tile([P, 2, P], U8, name="w_sd%d" % u, align_bytes=64) for u in range(2)]
+        w2_sd = [sb.tile([P, 2, P], U8, name="w2_sd%d" % u, align_bytes=64) for u in range(2)]
 
-        def deal(dst, src):
-            nc.vector.tensor_copy(out=dst, in_=src.rearrange("p (m t) -> p t m", t=PACK))
+        def dealt(src):
+            return src.rearrange("p (m t) -> p t m", t=PACK)
 
         nc.vector.tensor_copy(out=xg_w[:], in_=xt_w[:].indirect(tok_list[:]))
-        deal(w_wd[:].bitcast(I32), w_w[:].bitcast(I32))
         nc.vector.tensor_copy(out=xg_s[:], in_=xt_s[:].indirect(tok_list[:]))
-        deal(w2_wd[:].bitcast(I32), w2_w[:].bitcast(I32))
-        deal(w_sd[:], w_s[:])
-        deal(w2_sd[:], w2_s[:])
+        nc.vector.tensor_copy(out=w_wd[:].bitcast(I32), in_=dealt(w_w[:].bitcast(I32)))
+        nc.vector.tensor_copy(out=w2_wd[:].bitcast(I32), in_=dealt(w2_w[:].bitcast(I32)))
+        for planes, plane in ((w_sd, w_s), (w2_sd, w2_s)):
+            for u in range(2):
+                nc.vector.tensor_copy(out=planes[u][:], in_=dealt(plane[:])[:, 2 * u : 2 * u + 2, :])
 
         gate = [sb.tile([P, 2, J], F32, name="gate%d" % u) for u in range(2)]
 
@@ -102,60 +102,70 @@ def tile_list_twow_tablegate_one_plain_kernel(
                 scale=slope[:, t : t + 1],
             )
 
-        look(0)
-        look(1)
-
         a_ps = [ps.tile([P, 2, J], F32, name="a_ps%d" % u) for u in range(2)]
-        b_ps = [ps.tile([P, 2, J], F32, name="b_ps%d" % u) for u in range(2)]
-        a_sb = [sb.tile([P, 2, J], F32, name="a_sb%d" % u) for u in range(2)]
-        d_sb = [sb.tile([P, 2, J], F32, name="d_sb%d" % u) for u in range(2)]
-        mag = [sb.tile([P, J, 2], F32, name="mag%d" % u) for u in range(2)]
+        b_ps = [ps.tile([P, J], F32, name="b_ps%d" % t) for t in range(PACK)]
+        d_sb = [sb.tile([P, J], F32, name="d_sb%d" % t) for t in range(PACK)]
+        mag = [sb.tile([P, 2, J], F32, name="mag%d" % u) for u in range(2)]
         hid = sb.tile([P, J, PACK], BF16, name="hid", align_bytes=64)
 
-        for acc, words, plane, fmt in ((a_ps, w_wd, w_sd, E4M3), (b_ps, w2_wd, w2_sd, E5M2)):
-            for u in range(2):
-                for e in range(2):
-                    nc.tensor.matmul_mx(
-                        out=acc[u][:, e, :],
-                        lhsT=words[:, 2 * u + e, :].bitcast(fmt),
-                        lhsT_scale=plane[:, 2 * u + e, :],
-                        rhs=xg_w[:].bitcast(E2M1),
-                        rhs_scale=xg_s[:],
-                        start=True,
-                        stop=True,
-                    )
-        for u in range(2):
-            nc.scalar.copy(out=a_sb[u][:], in_=a_ps[u][:])
-        for u in range(2):
-            nc.vector.tensor_tensor(out=d_sb[u][:], in0=a_sb[u][:], in1=b_ps[u][:], op=ALU.subtract)
-            nc.scalar.activation(out=mag[u][:], in_=d_sb[u][:].rearrange("p e j -> p j e"), func=ACT.Abs)
-            look(2 + u)
-        for u in range(2):
-            nc.vector.tensor_tensor(
-                out=hid[:, :, 2 * u : 2 * u + 2],
-                in0=mag[u][:],
-                in1=gate[u][:].rearrange("p e j -> p j e"),
-                op=ALU.mult,
-            )
-        hq_w = sb.tile([P, J], U32, name="hq_w", align_bytes=64)
-        hq_s = sb.tile([P, J], U8, name="hq_s", align_bytes=64)
-        nc.vector.quantize_mx(out=hq_w[:].bitcast(E5M2), scales=hq_s[:], in_=hid[:].rearrange("p j t -> p (j t)"))
-
-        for h in range(2):
-            y_ps = ps.tile([P, J], F32, name="y_ps%d" % h)
-            y_sb = sb.tile([P, J], F32, name="y_sb%d" % h)
+        def first_stage(acc, words, planes, fmt, t):
             nc.tensor.matmul_mx(
-                out=y_ps[:],
-                lhsT=wb_w[:, 2 * h * P : 2 * (h + 1) * P].bitcast(E2M1),
-                lhsT_scale=wb_s[:, h * P : (h + 1) * P],
-                rhs=hq_w[:].bitcast(E5M2),
-                rhs_scale=hq_s[:],
+                out=acc,
+                lhsT=words[:, t, :].bitcast(fmt),
+                lhsT_scale=planes[t // 2][:, t % 2, :],
+                rhs=xg_w[:].bitcast(E2M1),
+                rhs_scale=xg_s[:],
                 start=True,
                 stop=True,
             )
+
+        look(0)
+        for t in range(PACK):
+            first_stage(a_ps[t // 2][:, t % 2, :], w_wd, w_sd, E4M3, t)
+        a_sb = sb.tile([P, PACK, J], F32, name="a_sb", tag="table0")
+        for u in range(2):
+            nc.scalar.copy(out=a_sb[:, 2 * u : 2 * u + 2, :], in_=a_ps[u][:])
+        look(1)
+        look(2)
+        for t in range(PACK):
+            first_stage(b_ps[t][:], w2_wd, w2_sd, E5M2, t)
+            nc.vector.tensor_tensor(out=d_sb[t][:], in0=a_sb[:, t, :], in1=b_ps[t][:], op=ALU.subtract)
+        for t in (0, 1):
+            nc.scalar.activation(out=mag[0][:, t, :], in_=d_sb[t][:], func=ACT.Abs)
+        nc.vector.scalar_tensor_tensor(
+            out=mag[1][:, 1, :], in0=d_sb[3][:], scalar=-1.0, in1=d_sb[3][:], op0=ALU.mult, op1=ALU.max
+        )
+        look(3)
+        nc.scalar.activation(out=mag[1][:, 0, :], in_=d_sb[2][:], func=ACT.Abs)
+        for u, cols in ((0, slice(0, J)), (1, slice(0, P)), (1, slice(P, J))):
+            nc.vector.tensor_tensor(
+                out=hid[:, cols, 2 * u : 2 * u + 2],
+                in0=mag[u][:, :, cols].rearrange("p e j -> p j e"),
+                in1=gate[u][:, :, cols].rearrange("p e j -> p j e"),
+                op=ALU.mult,
+            )
+        out_rows = out.rearrange("(g p) j -> p g j", p=P)
+        for h in range(2):
+            hq_w = sb.tile([P, P], U32, name="hq_w%d" % h, align_bytes=64)
+            hq_s = sb.tile([P, P], U8, name="hq_s%d" % h, align_bytes=64)
+            nc.vector.quantize_mx(
+                out=hq_w[:].bitcast(E5M2), scales=hq_s[:], in_=hid[:, h * P : (h + 1) * P, :].rearrange("p j t -> p (j t)")
+            )
+            y_ps = ps.tile([P, 2, P], F32, name="y_ps%d" % h)
+            y_sb = sb.tile([P, 2, P], F32, name="y_sb%d" % h)
+            for g in range(2):
+                nc.tensor.matmul_mx(
+                    out=y_ps[:, g, :],
+                    lhsT=wb_w[:, 2 * g * P : 2 * (g + 1) * P].bitcast(E2M1),
+                    lhsT_scale=wb_s[:, g * P : (g + 1) * P],
+                    rhs=hq_w[:].bitcast(E5M2),
+                    rhs_scale=hq_s[:],
+                    start=True,
+                    stop=True,
+                )
             if h == 0:
-                nc.vector.tensor_copy(out=y_sb[:], in_=y_ps[:])
-                nc.sync.dma_start(out=out[h * P : (h + 1) * P, :], in_=y_sb[:])
-            else:
                 nc.scalar.copy(out=y_sb[:], in_=y_ps[:])
-                nc.scalar.dma_start(out=out[h * P : (h + 1) * P, :], in_=y_sb[:])
+                nc.scalar.dma_start(out=out_rows[:, :, h * P : (h + 1) * P], in_=y_sb[:])
+            else:
+                nc.vector.tensor_copy(out=y_sb[:], in_=y_ps[:])
+                nc.sync.dma_start(out=out_rows[:, :, h * P : (h + 1) * P], in_=y_sb[:])

@@ -77,19 +77,18 @@ def tile_list_twow_tablegate_one_plain_kernel(
         xg_s = sb.tile([P, J], U8, name="xg_s", align_bytes=64)
         w_wd = sb.tile([P, PACK, P], U32, name="w_wd", align_bytes=64)
         w2_wd = sb.tile([P, PACK, P], U32, name="w2_wd", align_bytes=64)
-        w_sd = [sb.tile([P, 2, P], U8, name="w_sd%d" % u, align_bytes=64) for u in range(2)]
-        w2_sd = [sb.tile([P, 2, P], U8, name="w2_sd%d" % u, align_bytes=64) for u in range(2)]
+        w_sd = sb.tile([P, PACK, P], U8, name="w_sd", align_bytes=64)
+        w2_sd = sb.tile([P, PACK, P], U8, name="w2_sd", align_bytes=64)
 
-        def dealt(src):
-            return src.rearrange("p (m t) -> p t m", t=PACK)
+        def deal(dst, src):
+            nc.vector.tensor_copy(out=dst.rearrange("p t m -> p m t"), in_=src.rearrange("p (m t) -> p m t", t=PACK))
 
         nc.vector.tensor_copy(out=xg_w[:], in_=xt_w[:].indirect(tok_list[:]))
         nc.vector.tensor_copy(out=xg_s[:], in_=xt_s[:].indirect(tok_list[:]))
-        nc.vector.tensor_copy(out=w_wd[:].bitcast(I32), in_=dealt(w_w[:].bitcast(I32)))
-        nc.vector.tensor_copy(out=w2_wd[:].bitcast(I32), in_=dealt(w2_w[:].bitcast(I32)))
-        for planes, plane in ((w_sd, w_s), (w2_sd, w2_s)):
-            for u in range(2):
-                nc.vector.tensor_copy(out=planes[u][:], in_=dealt(plane[:])[:, 2 * u : 2 * u + 2, :])
+        deal(w_wd[:].bitcast(I32), w_w[:].bitcast(I32))
+        deal(w_sd[:], w_s[:])
+        deal(w2_wd[:].bitcast(I32), w2_w[:].bitcast(I32))
+        deal(w2_sd[:], w2_s[:])
 
         gate = [sb.tile([P, 2, J], F32, name="gate%d" % u) for u in range(2)]
 
@@ -112,7 +111,7 @@ def tile_list_twow_tablegate_one_plain_kernel(
             nc.tensor.matmul_mx(
                 out=acc,
                 lhsT=words[:, t, :].bitcast(fmt),
-                lhsT_scale=planes[t // 2][:, t % 2, :],
+                lhsT_scale=planes[:, t, :],
                 rhs=xg_w[:].bitcast(E2M1),
                 rhs_scale=xg_s[:],
                 start=True,
@@ -163,9 +162,5 @@ def tile_list_twow_tablegate_one_plain_kernel(
                     start=True,
                     stop=True,
                 )
-            if h == 0:
-                nc.scalar.copy(out=y_sb[:], in_=y_ps[:])
-                nc.scalar.dma_start(out=out_rows[:, :, h * P : (h + 1) * P], in_=y_sb[:])
-            else:
-                nc.vector.tensor_copy(out=y_sb[:], in_=y_ps[:])
-                nc.sync.dma_start(out=out_rows[:, :, h * P : (h + 1) * P], in_=y_sb[:])
+            nc.scalar.copy(out=y_sb[:], in_=y_ps[:])
+            (nc.sync, nc.scalar)[h].dma_start(out=out_rows[:, :, h * P : (h + 1) * P], in_=y_sb[:])

from contextlib import ExitStack

import concourse.mybir as mybir

K, T, J, R, Q, N = 512, 1024, 256, 512, 1024, 256
FLOPS = 2 * (2 * K * R * J + R * N * J)

F32 = mybir.dt.float32
BF16 = mybir.dt.bfloat16
I32 = mybir.dt.int32
U32 = mybir.dt.uint32
U16 = mybir.dt.uint16
U8 = mybir.dt.uint8
E4M3 = mybir.dt.float8_e4m3fn_x4
E5M2 = mybir.dt.float8_e5m2_x4
E2M1 = mybir.dt.float4_e2m1fn_x4
ACT = mybir.ActivationFunctionType
ALU = mybir.AluOpType

P = 128
PACK = 4


def load_scales(queue, plane, rows, which=range(4)):
    for r in which:
        queue.dma_start(out=plane[r:P:32, :].bitcast(I32), in_=rows[0, r:16:4, :].bitcast(I32))


def tile_list_twow_tablegate_one_plain_kernel(
    tc, xt_words, xt_scales, w_words, w_scales, w2_words, w2_scales, tg, sg, bg, wb_words, wb_scales, offs, offs2, out
):
    nc = tc.nc
    with ExitStack() as ctx:
        sb = ctx.enter_context(tc.tile_pool(name="sb", bufs=1))
        ps = ctx.enter_context(tc.psum_pool(name="ps", bufs=1))

        tok_list = sb.tile([P, J // 16], U16, name="tok_list")
        gate_list = sb.tile([P, J // 16], U16, name="gate_list")
        xt_w = sb.tile([P, T], U16, name="xt_w", align_bytes=64)
        xt_s = sb.tile([P, T], U8, name="xt_s", align_bytes=64)
        w_w = sb.tile([P, R], U32, name="w_w", align_bytes=64)
        w_s = sb.tile([P, R], U8, name="w_s", align_bytes=64)
        w2_w = sb.tile([P, R], U32, name="w2_w", align_bytes=64)
        w2_s = sb.tile([P, R], U8, name="w2_s", align_bytes=64)
        wb_w = sb.tile([P, 2 * N], U8, name="wb_w", align_bytes=64)
        wb_s = sb.tile([P, N], U8, name="wb_s", align_bytes=64)
        slope = sb.tile([P, PACK], F32, name="slope")
        offset = sb.tile([P, PACK], F32, name="offset")
        table = [sb.tile([P, Q], F32, name="table%d" % t, tag="table%d" % t) for t in range(PACK)]

        warm_in = sb.tile([P, 1], F32, name="warm_in")
        warm_out = sb.tile([P, 1], F32, name="warm_out")
        nc.gpsimd.memset(warm_in[:], 0.0)
        nc.scalar.activation(out=warm_out[:], in_=warm_in[:], func=ACT.Sigmoid)
        for plane in (xt_s, w_s, w2_s, wb_s):
            nc.vector.memset(plane[:].bitcast(I32), 0)

        tg_rows = tg.rearrange("(p t) q -> p t q", t=PACK)
        nc.gpsimd.dma_start(out=slope[:], in_=sg.rearrange("(p t) o -> p (t o)", t=PACK))
        nc.gpsimd.dma_start(out=offset[:], in_=bg.rearrange("(p t) o -> p (t o)", t=PACK))
        nc.sync.dma_start(out=xt_w[:].bitcast(I32), in_=xt_words[0].bitcast(I32))
        nc.sync.dma_start(tok_list[:], offs)
        load_scales(nc.sync, xt_s, xt_scales)
        nc.sync.dma_start(out=w_w[:].bitcast(I32), in_=w_words[0].rearrange("p n t -> p (n t)").bitcast(I32))
        nc.sync.dma_start(out=table[0][:], in_=tg_rows[:, 0, :])
        load_scales(nc.sync, w_s, w_scales)
        nc.sync.dma_start(out=w2_w[:].bitcast(I32), in_=w2_words[0].rearrange("p n t -> p (n t)").bitcast(I32))
        nc.sync.dma_start(gate_list[:], offs2)
        nc.sync.dma_start(out=table[1][:], in_=tg_rows[:, 1, :])
        load_scales(nc.sync, w2_s, w2_scales)
        nc.sync.dma_start(out=table[2][:], in_=tg_rows[:, 2, :])
        nc.sync.dma_start(out=table[3][:], in_=tg_rows[:, 3, :])
        nc.sync.dma_start(out=wb_w[:].bitcast(I32), in_=wb_words[0].bitcast(I32))
        load_scales(nc.sync, wb_s, wb_scales)

        xg_w = sb.tile([P, J], U16, name="xg_w", align_bytes=64)
        xg_s = sb.tile([P, J], U8, name="xg_s", align_bytes=64)
        w_wd = sb.tile([P, PACK, P], U32, name="w_wd", align_bytes=64)
        w2_wd = sb.tile([P, PACK, P], U32, name="w2_wd", align_bytes=64)
        w_sd = sb.tile([P, PACK, P], U8, name="w_sd", align_bytes=64)
        w2_sd = sb.tile([P, PACK, P], U8, name="w2_sd", align_bytes=64)

        def deal(dst, src):
            nc.vector.tensor_copy(out=dst.rearrange("p t m -> p m t"), in_=src.rearrange("p (m t) -> p m t", t=PACK))

        nc.vector.tensor_copy(out=xg_w[:], in_=xt_w[:].indirect(tok_list[:]))
        nc.vector.tensor_copy(out=xg_s[:], in_=xt_s[:].indirect(tok_list[:]))
        deal(w_wd[:].bitcast(I32), w_w[:].bitcast(I32))
        deal(w_sd[:], w_s[:])
        deal(w2_wd[:].bitcast(I32), w2_w[:].bitcast(I32))
        deal(w2_sd[:], w2_s[:])

        gate = [sb.tile([P, 2, J], F32, name="gate%d" % u) for u in range(2)]

        def look(t):
            nc.scalar.activation(
                out=gate[t // 2][:, t % 2, :],
                in_=table[t][:].indirect(gate_list[:]),
                func=ACT.Sigmoid,
                bias=offset[:, t : t + 1],
                scale=slope[:, t : t + 1],
            )

        a_ps = [ps.tile([P, 2, J], F32, name="a_ps%d" % u) for u in range(2)]
        b_ps = [ps.tile([P, J], F32, name="b_ps%d" % t) for t in range(PACK)]
        d_sb = [sb.tile([P, J], F32, name="d_sb%d" % t) for t in range(PACK)]
        mag = [sb.tile([P, 2, J], F32, name="mag%d" % u) for u in range(2)]
        hid = sb.tile([P, J, PACK], BF16, name="hid", align_bytes=64)

        def first_stage(acc, words, planes, fmt, t):
            nc.tensor.matmul_mx(
                out=acc,
                lhsT=words[:, t, :].bitcast(fmt),
                lhsT_scale=planes[:, t, :],
                rhs=xg_w[:].bitcast(E2M1),
                rhs_scale=xg_s[:],
                start=True,
                stop=True,
            )

        look(0)
        for t in range(PACK):
            first_stage(a_ps[t // 2][:, t % 2, :], w_wd, w_sd, E4M3, t)
        a_sb = sb.tile([P, PACK, J], F32, name="a_sb", tag="table0")
        for u in range(2):
            nc.scalar.copy(out=a_sb[:, 2 * u : 2 * u + 2, :], in_=a_ps[u][:])
        look(1)
        look(2)
        for t in range(PACK):
            first_stage(b_ps[t][:], w2_wd, w2_sd, E5M2, t)
            nc.vector.tensor_tensor(out=d_sb[t][:], in0=a_sb[:, t, :], in1=b_ps[t][:], op=ALU.subtract)
        for t in (0, 1):
            nc.scalar.activation(out=mag[0][:, t, :], in_=d_sb[t][:], func=ACT.Abs)
        nc.vector.scalar_tensor_tensor(
            out=mag[1][:, 1, :], in0=d_sb[3][:], scalar=-1.0, in1=d_sb[3][:], op0=ALU.mult, op1=ALU.max
        )
        look(3)
        nc.scalar.activation(out=mag[1][:, 0, :], in_=d_sb[2][:], func=ACT.Abs)
        for u, cols in ((0, slice(0, J)), (1, slice(0, P)), (1, slice(P, J))):
            nc.vector.tensor_tensor(
                out=hid[:, cols, 2 * u : 2 * u + 2],
                in0=mag[u][:, :, cols].rearrange("p e j -> p j e"),
                in1=gate[u][:, :, cols].rearrange("p e j -> p j e"),
                op=ALU.mult,
            )
        out_rows = out.rearrange("(g p) j -> p g j", p=P)
        for h in range(2):
            hq_w = sb.tile([P, P], U32, name="hq_w%d" % h, align_bytes=64)
            hq_s = sb.tile([P, P], U8, name="hq_s%d" % h, align_bytes=64)
            nc.vector.quantize_mx(
                out=hq_w[:].bitcast(E5M2), scales=hq_s[:], in_=hid[:, h * P : (h + 1) * P, :].rearrange("p j t -> p (j t)")
            )
            y_ps = ps.tile([P, 2, P], F32, name="y_ps%d" % h)
            y_sb = sb.tile([P, 2, P], F32, name="y_sb%d" % h)
            for g in range(2):
                nc.tensor.matmul_mx(
                    out=y_ps[:, g, :],
                    lhsT=wb_w[:, 2 * g * P : 2 * (g + 1) * P].bitcast(E2M1),
                    lhsT_scale=wb_s[:, g * P : (g + 1) * P],
                    rhs=hq_w[:].bitcast(E5M2),
                    rhs_scale=hq_s[:],
                    start=True,
                    stop=True,
                )
            nc.scalar.copy(out=y_sb[:], in_=y_ps[:])
            (nc.sync, nc.scalar)[h].dma_start(out=out_rows[:, :, h * P : (h + 1) * P], in_=y_sb[:])
